import numpy as np
import ml_dtypes


def mxq(x, axis, fmt="e4m3"):
    dtype, down = {"e4m3": (ml_dtypes.float8_e4m3fn, 7), "e5m2": (ml_dtypes.float8_e5m2, 14)}[fmt]
    v = np.moveaxis(np.asarray(x, np.float32).astype(ml_dtypes.bfloat16).astype(np.float64), axis, -1)
    blocks = v.reshape(v.shape[:-1] + (-1, 32))
    amax = np.abs(blocks).max(-1, keepdims=True)
    byte = np.maximum(np.where(amax > 0, np.frexp(amax)[1] - 1 + 127, 0) - down, 1)
    scale = np.exp2(byte - 127.0)
    codes = (blocks / scale).astype(np.float32).astype(dtype).astype(np.float64)
    return np.moveaxis((codes * scale).reshape(v.shape), -1, axis)


WIDE = False


def mx_kscale(k):
    if not WIDE:
        return np.ones(k)
    levels = np.array([10, -10, 5, -5, 0])
    if k % 512:
        return np.exp2(np.random.permutation(np.resize(levels, k // 32))).repeat(32)
    a = np.empty((k // 512, 16))
    for p in range(k // 512):
        a[p, :8] = np.random.permutation(np.resize(levels, 8))
        for g in range(8):
            far = levels[np.abs(levels - a[p, g]) >= 10]
            a[p, g + 8] = far[np.random.randint(len(far))]
    return np.exp2(a.ravel()).repeat(32)


def f64(x):
    return np.asarray(x).astype(np.float64)


def striped8(idx):
    return np.asarray(idx).reshape(8, -1, 16).transpose(0, 2, 1).reshape(128, -1).astype(np.uint16)


def unstriped8(offs):
    return offs.reshape(8, 16, -1).transpose(0, 2, 1).reshape(8, -1).astype(np.int64)


def pick8(x, idx, run):
    r = np.arange(len(x))
    return x[r[:, None], idx[r % (8 * run) // run]]


E2M1 = np.array([0.0, 0.5, 1.0, 1.5, 2.0, 3.0, 4.0, 6.0, -0.0, -0.5, -1.0, -1.5, -2.0, -3.0, -4.0, -6.0])


def pack_weight(w, fmt):
    k, n = w.shape
    w = f64(np.asarray(w, np.float32).astype(ml_dtypes.bfloat16)).reshape(k // 32, 32, n)
    amax = np.abs(w).max(1)
    if fmt == "e4m3":
        byte = np.frexp(amax)[1] - 1 + 127 - 7
    else:
        mant, ex = np.frexp(amax / 6.0)
        byte = np.where(mant > 0.5, ex, ex - 1) + 127
    byte = np.clip(np.where(amax > 0, byte, 1), 1, 254)
    scaled = (w * np.exp2(127.0 - byte)[:, None, :]).reshape(k, n).astype(np.float32)
    by_word = np.ascontiguousarray(scaled.reshape(k // 512, 128, 4, n).transpose(0, 1, 3, 2))
    if fmt == "e4m3":
        words = by_word.astype(ml_dtypes.float8_e4m3fn).view(np.uint8)
    else:
        c = by_word.astype(ml_dtypes.float4_e2m1fn).view(np.uint8) & 0xF
        words = (c[..., 0::2] | (c[..., 1::2] << 4)).reshape(k // 512, 128, 2 * n)
    return np.ascontiguousarray(words), np.ascontiguousarray(byte.astype(np.uint8).reshape(k // 512, 16, n))


def unpack_weight(words, scales, fmt):
    g, _, n = scales.shape
    words = np.ascontiguousarray(words).reshape(g, 128, n, -1)
    if fmt == "e4m3":
        vals = words.view(ml_dtypes.float8_e4m3fn).astype(np.float64)
    else:
        nib = np.empty((g, 128, n, 4), np.uint8)
        nib[..., 0::2] = words & 0xF
        nib[..., 1::2] = words >> 4
        vals = E2M1[nib]
    vals = vals * np.repeat(np.exp2(scales.astype(np.float64) - 127.0), 8, axis=1)[..., None]
    return vals.transpose(0, 1, 3, 2).reshape(g * 512, n)


def sigmoid(v):
    return 1.0 / (1.0 + np.exp(-v))


D, V, Q, I = 512, 2048, 128, 512


def setup_inputs():
    n = np.random.standard_normal
    idx = np.stack([np.random.permutation(V)[:I] for _ in range(8)])
    idx2 = np.stack([np.random.permutation(V)[:I] for _ in range(8)])
    fd = mx_kscale(D)
    vocp = pack_weight(n((D, V)) / fd[:, None], "e4m3")
    return {
        "hid": (n((D, Q)) * 1.0 / np.sqrt(D) * fd[:, None]).astype(np.float32),
        "voc_words": vocp[0],
        "voc_scales": vocp[1],
        "sw": (np.random.uniform(0.5, 2.0, (1, I))).astype(np.float32),
        "old": (0.5 * n((Q, V))).astype(np.float32),
        "offs": striped8(idx),
        "offs2": striped8(idx2),
    }


def reference(hid, voc_words, voc_scales, sw, old, offs, offs2):
    idx = unstriped8(offs)
    idx2 = unstriped8(offs2)
    vocu = unpack_weight(voc_words, voc_scales, "e4m3")
    hidq = mxq(f64(hid), 0, "e4m3")
    a = hidq.T @ vocu
    m1 = np.max(a, axis=1, keepdims=True)
    p = np.exp(a - m1)
    z = np.sum(p, axis=1, keepdims=True)
    px = np.exp(pick8(a, idx, 16) - m1)
    px2 = np.exp(pick8(a, idx2, 16) - m1)
    u1 = sigmoid((px2 - px) / z * 512.0)
    dpx2 = f64(sw) * u1 * (1.0 - u1) * 512.0 / z
    dpx = f64(sw) * u1 * (1.0 - u1) * 512.0 / z * (-1.0)
    dz = np.sum(f64(sw) * u1 * (1.0 - u1) * 512.0 * (px2 - px) / np.square(z) * (-1.0), axis=1, keepdims=True)
    e1 = dpx2 * px2
    s1 = np.zeros((Q, V))
    s1[np.arange(Q)[:, None], idx2[np.arange(Q) % 128 // 16]] = e1
    e2 = dpx * px
    s2 = np.zeros((Q, V))
    s2[np.arange(Q)[:, None], idx[np.arange(Q) % 128 // 16]] = e2
    da = dz * p + s1 + s2
    y = da * 2.0 + f64(old)
    return y

@@ -1,0 +1,204 @@
+from contextlib import ExitStack
+
+import concourse.mybir as mybir
+from concourse.masks import make_identity
+
+D, V, Q, SLOTS = 512, 2048, 128, 512
+FLOPS = 2 * D * V * Q
+
+F32 = mybir.dt.float32
+BF16 = mybir.dt.bfloat16
+I32 = mybir.dt.int32
+U32 = mybir.dt.uint32
+U16 = mybir.dt.uint16
+U8 = mybir.dt.uint8
+FP8X4 = mybir.dt.float8_e4m3fn_x4
+ALU = mybir.AluOpType
+ACT = mybir.ActivationFunctionType
+AX = mybir.AxisListType
+
+P = 128
+PACK = 4
+BANK = 512
+NBANK = V // BANK
+WORD_LOADS = ((0, 512), (512, 1024), (1024, 2048))
+CHUNKS = ((0, 256), (256, 512), (512, 1024), (1024, 1536), (1536, 2048))
+HALVES = ((0, 256), (256, 512))
+
+
+def tile_attend_brankshares_heads_kernel(tc, hid, voc_words, voc_scales, sw, old, offs, offs2, out):
+    nc = tc.nc
+    nch = len(CHUNKS)
+    with ExitStack() as ctx:
+        keep = ctx.enter_context(tc.tile_pool(name="keep", bufs=1))
+        psum = ctx.enter_context(tc.psum_pool(name="psum", bufs=1))
+
+        planes = keep.tile([P, BANK], U8, align_bytes=64)
+        nc.vector.memset(planes[:].bitcast(U32), 0)
+
+        raw = keep.tile([P, PACK, Q], F32, tag="raw")
+        nc.sync.dma_start(out=raw[:], in_=hid.rearrange("(p j) q -> p j q", j=PACK))
+        for quad in range(4):
+            rows = voc_scales[0][4 * quad : 4 * quad + 4, :].bitcast(I32)
+            nc.sync.dma_start(
+                out=planes[32 * quad : 32 * quad + 16, :].bitcast(I32),
+                in_=rows.rearrange("r (c n) -> c r n", c=NBANK),
+            )
+        flat_words = voc_words[0].rearrange("p n t -> p (n t)")
+        words = []
+        for lo, hi in WORD_LOADS:
+            w = keep.tile([P, hi - lo], U32, align_bytes=64, name="words%d" % lo)
+            nc.sync.dma_start(out=w[:].bitcast(I32), in_=flat_words[:, PACK * lo : PACK * hi].bitcast(I32))
+            words.append((lo, hi, w))
+        list1 = keep.tile([P, SLOTS // 16], U16)
+        nc.sync.dma_start(list1[:], offs)
+        list2 = keep.tile([P, SLOTS // 16], U16)
+        nc.sync.dma_start(list2[:], offs2)
+
+        up = keep.tile([P, V], F32)
+        nc.vector.memset(up[:], 0.0)
+        fac = keep.tile([P, nch], F32)
+        nc.vector.memset(fac[:, nch - 1 : nch], 1.0)
+        ident = keep.tile([P, P], F32)
+        make_identity(nc, ident[:])
+
+        grouped = keep.tile([P, Q, PACK], BF16, align_bytes=64, tag="grouped")
+        nc.vector.tensor_copy(out=grouped[:], in_=raw[:].rearrange("p j q -> p q j"))
+        hcodes = keep.tile([P, Q], U32, align_bytes=64)
+        hscales = keep.tile([P, Q], U8, align_bytes=64)
+        nc.vector.quantize_mx(
+            out=hcodes[:].bitcast(FP8X4), scales=hscales[:], in_=grouped[:].rearrange("p q j -> p (q j)")
+        )
+
+        sw_col = keep.tile([P, PACK], F32, tag="raw")
+        nc.gpsimd.dma_start(out=sw_col[:], in_=sw[0].rearrange("(p c) -> p c", c=PACK))
+        old_sb = keep.tile([P, V], F32, align_bytes=64, tag="grouped")
+        nc.sync.dma_start(out=old_sb[:], in_=old)
+
+        a_sb = keep.tile([P, V], F32)
+        p_sb = keep.tile([P, V], F32)
+        mx = keep.tile([P, nch], F32)
+        neg = keep.tile([P, nch - 1], F32, tag="neg")
+        neg_m = keep.tile([P, 1], F32)
+        zc = keep.tile([P, nch], F32)
+        for c, (lo, hi) in enumerate(CHUNKS):
+            wlo, whi, w = [t for t in words if t[0] <= lo and hi <= t[1]][0]
+            b = lo // BANK
+            acc = psum.tile([P, hi - lo], F32, tag="bank%d" % c, name="acc%d" % c)
+            nc.tensor.matmul_mx(
+                out=acc[:],
+                lhsT=hcodes[:].bitcast(FP8X4),
+                lhsT_scale=hscales[:],
+                rhs=w[:, lo - wlo : hi - wlo].bitcast(FP8X4),
+                rhs_scale=planes[4 * b :, lo - b * BANK : hi - b * BANK],
+                start=True,
+                stop=True,
+            )
+            nc.vector.tensor_scalar(
+                a_sb[:, lo:hi], acc[:], 1.0, None, ALU.mult, ALU.max, accum_out=mx[:, c : c + 1]
+            )
+            if c < nch - 1:
+                nc.gpsimd.tensor_scalar(neg[:, c : c + 1], mx[:, c : c + 1], -1.0, 0.0, ALU.mult, ALU.add)
+                bias = neg[:, c : c + 1]
+            else:
+                nc.vector.tensor_reduce(neg_m[:], mx[:], AX.X, ALU.max, negate=True)
+                bias = neg_m[:]
+            nc.scalar.activation(p_sb[:, lo:hi], a_sb[:, lo:hi], ACT.Exp, bias=bias, accum_out=zc[:, c : c + 1])
+
+        down = keep.tile([P, V], F32, tag="neg")
+        nc.gpsimd.memset(down[:], 0.0)
+        nc.scalar.activation(fac[:, : nch - 1], mx[:, : nch - 1], ACT.Exp, bias=neg_m[:])
+        px2 = keep.tile([P, SLOTS], F32)
+        nc.scalar.activation(px2[:], a_sb[:].indirect(list2[:]), ACT.Exp, bias=neg_m[:])
+        a1 = keep.tile([P, SLOTS], F32)
+        nc.vector.tensor_copy(a1[:], a_sb[:].indirect(list1[:]))
+
+        sw_ps = psum.tile([P, PACK, P], F32, tag="bank5")
+        for c in range(PACK):
+            nc.tensor.transpose(sw_ps[:, c, :], sw_col[:, c : c + 1].to_broadcast([P, P]), ident[:])
+
+        zf = keep.tile([P, nch], F32)
+        z256 = keep.tile([P, 1], F32)
+        nc.vector.scalar_tensor_tensor(zf[:], zc[:], 1.0 / 256.0, fac[:], ALU.mult, ALU.mult, accum_out=z256[:])
+        k = keep.tile([P, 1], F32)
+        nc.vector.reciprocal(k[:], z256[:])
+        swk = keep.tile([P, P, PACK], F32)
+        nc.vector.tensor_scalar(swk[:], sw_ps[:].rearrange("q c p -> q p c"), k[:], -1.0, ALU.mult, ALU.mult)
+        swk_flat = swk[:].rearrange("q p c -> q (p c)")
+        fk = keep.tile([P, nch], F32)
+        nc.vector.tensor_scalar(fk[:], fac[:], k[:], -1.0 / 256.0, ALU.mult, ALU.mult)
+
+        px = keep.tile([P, SLOTS], F32)
+        diff = keep.tile([P, SLOTS], F32)
+        th = keep.tile([P, SLOTS], F32)
+        sq = keep.tile([P, SLOTS], F32)
+        g = keep.tile([P, SLOTS], F32)
+        gd = keep.tile([P, SLOTS], F32)
+        rr = keep.tile([P, len(HALVES)], F32)
+        for lo, hi in HALVES:
+            nc.scalar.activation(px[:, lo:hi], a1[:, lo:hi], ACT.Exp, bias=neg_m[:])
+            nc.vector.tensor_tensor(diff[:, lo:hi], px2[:, lo:hi], px[:, lo:hi], ALU.subtract)
+        wd = keep.tile([P, SLOTS], F32)
+        for lo, hi in HALVES:
+            nc.vector.tensor_tensor(wd[:, lo:hi], diff[:, lo:hi], swk_flat[:, lo:hi], ALU.mult)
+        for h, (lo, hi) in enumerate(HALVES):
+            nc.scalar.activation(th[:, lo:hi], diff[:, lo:hi], ACT.Tanh, scale=k[:])
+            nc.scalar.activation(sq[:, lo:hi], th[:, lo:hi], ACT.Square)
+            nc.vector.scalar_tensor_tensor(
+                g[:, lo:hi], sq[:, lo:hi], -1.0, swk_flat[:, lo:hi], ALU.add, ALU.mult
+            )
+            nc.vector.scalar_tensor_tensor(
+                gd[:, lo:hi], sq[:, lo:hi], -1.0, wd[:, lo:hi], ALU.add, ALU.mult, accum_out=rr[:, h : h + 1]
+            )
+        nc.vector.tensor_tensor(up[:].indirect(list2[:]), g[:], px2[:], ALU.mult)
+        nc.vector.tensor_tensor(down[:].indirect(list1[:]), g[:], px[:], ALU.mult)
+
+        r = keep.tile([P, 1], F32)
+        nc.scalar.activation(r[:], rr[:, 0:1], ACT.Identity, bias=rr[:, 1:2])
+        cvec = keep.tile([P, nch], F32)
+        nc.scalar.activation(cvec[:], fk[:], ACT.Copy, scale=r[:])
+        cp = keep.tile([P, V], F32)
+        for c, (lo, hi) in enumerate(CHUNKS):
+            nc.scalar.activation(cp[:, lo:hi], p_sb[:, lo:hi], ACT.Copy, scale=cvec[:, c : c + 1])
+
+        turned = [psum.tile([P, BANK], F32, tag="bank%d" % ((6 + b) % 8), name="turned%d" % b) for b in range(NBANK)]
+
+        def blocks(b):
+            return [3 * b, 3 * b + 1, 3 * b + 2, 12 + b]
+
+        def add_turned(src, b, places, first, last):
+            for j in places:
+                blk = blocks(b)[j]
+                nc.tensor.matmul(
+                    turned[b][:, j * P : (j + 1) * P],
+                    lhsT=src[:, blk * P : (blk + 1) * P],
+                    rhs=ident[:],
+                    is_transpose=True,
+                    start=(first and j == 0),
+                    stop=(last and j == 3),
+                )
+
+        for b in range(NBANK):
+            add_turned(old_sb, b, range(4), True, False)
+        for b in range(NBANK):
+            add_turned(cp, b, range(3), False, False)
+        for b in range(NBANK):
+            add_turned(cp, b, (3,), False, False)
+        res_last = [keep.tile([P, 2 * P], F32, name="res_last%d" % h) for h in range(2)]
+        for b in range(NBANK):
+            add_turned(up, b, range(4), False, True)
+            turned_sb = keep.tile([P, BANK], F32, name="turned_sb%d" % b)
+            nc.scalar.copy(turned_sb[:], turned[b][:])
+            back = psum.tile([P, BANK], F32, tag="bank%d" % (2 + b), name="back%d" % b)
+            for j in range(BANK // P):
+                nc.tensor.transpose(back[:, j * P : (j + 1) * P], turned_sb[:, j * P : (j + 1) * P], ident[:])
+            lo = (12 + b) * P
+            nc.vector.tensor_tensor(
+                res_last[b // 2][:, (b % 2) * P : (b % 2 + 1) * P], back[:, 3 * P :], down[:, lo : lo + P], ALU.subtract
+            )
+            if b % 2 == 1:
+                nc.sync.dma_start(out=out[:, lo - P : lo + P], in_=res_last[b // 2][:])
+            res = keep.tile([P, 3 * P], F32, name="res%d" % b)
+            lo = 3 * b * P
+            nc.vector.tensor_tensor(res[:], back[:, : 3 * P], down[:, lo : lo + 3 * P], ALU.subtract)
+            nc.sync.dma_start(out=out[:, lo : lo + 3 * P], in_=res[:])

@@ -56,7 +56,9 @@ def tile_attend_brankshares_heads_kernel(tc, hid, voc_words, voc_scales, sw, old
         nc.sync.dma_start(list2[:], offs2)
 
         up = keep.tile([P, V], F32)
+        down = keep.tile([P, V], F32)
         nc.vector.memset(up[:], 0.0)
+        nc.vector.memset(down[:], 0.0)
         fac = keep.tile([P, nch], F32)
         nc.vector.memset(fac[:, nch - 1 : nch], 1.0)
         ident = keep.tile([P, P], F32)
@@ -71,14 +73,14 @@ def tile_attend_brankshares_heads_kernel(tc, hid, voc_words, voc_scales, sw, old
         )
 
         sw_col = keep.tile([P, PACK], F32, tag="raw")
-        nc.gpsimd.dma_start(out=sw_col[:], in_=sw[0].rearrange("(p c) -> p c", c=PACK))
+        nc.sync.dma_start(out=sw_col[:], in_=sw[0].rearrange("(p c) -> p c", c=PACK))
         old_sb = keep.tile([P, V], F32, align_bytes=64, tag="grouped")
         nc.sync.dma_start(out=old_sb[:], in_=old)
 
         a_sb = keep.tile([P, V], F32)
         p_sb = keep.tile([P, V], F32)
         mx = keep.tile([P, nch], F32)
-        neg = keep.tile([P, nch - 1], F32, tag="neg")
+        neg = keep.tile([P, nch - 1], F32)
         neg_m = keep.tile([P, 1], F32)
         zc = keep.tile([P, nch], F32)
         for c, (lo, hi) in enumerate(CHUNKS):
@@ -105,8 +107,6 @@ def tile_attend_brankshares_heads_kernel(tc, hid, voc_words, voc_scales, sw, old
                 bias = neg_m[:]
             nc.scalar.activation(p_sb[:, lo:hi], a_sb[:, lo:hi], ACT.Exp, bias=bias, accum_out=zc[:, c : c + 1])
 
-        down = keep.tile([P, V], F32, tag="neg")
-        nc.gpsimd.memset(down[:], 0.0)
         nc.scalar.activation(fac[:, : nch - 1], mx[:, : nch - 1], ACT.Exp, bias=neg_m[:])
         px2 = keep.tile([P, SLOTS], F32)
         nc.scalar.activation(px2[:], a_sb[:].indirect(list2[:]), ACT.Exp, bias=neg_m[:])
@@ -192,13 +192,13 @@ def tile_attend_brankshares_heads_kernel(tc, hid, voc_words, voc_scales, sw, old
             back = psum.tile([P, BANK], F32, tag="bank%d" % (2 + b), name="back%d" % b)
             for j in range(BANK // P):
                 nc.tensor.transpose(back[:, j * P : (j + 1) * P], turned_sb[:, j * P : (j + 1) * P], ident[:])
+            res = keep.tile([P, 3 * P], F32, name="res%d" % b)
+            lo = 3 * b * P
+            nc.vector.tensor_tensor(res[:], back[:, : 3 * P], down[:, lo : lo + 3 * P], ALU.subtract)
+            nc.sync.dma_start(out=out[:, lo : lo + 3 * P], in_=res[:])
             lo = (12 + b) * P
             nc.vector.tensor_tensor(
                 res_last[b // 2][:, (b % 2) * P : (b % 2 + 1) * P], back[:, 3 * P :], down[:, lo : lo + P], ALU.subtract
             )
             if b % 2 == 1:
                 nc.sync.dma_start(out=out[:, lo - P : lo + P], in_=res_last[b // 2][:])
-            res = keep.tile([P, 3 * P], F32, name="res%d" % b)
-            lo = 3 * b * P
-            nc.vector.tensor_tensor(res[:], back[:, : 3 * P], down[:, lo : lo + 3 * P], ALU.subtract)
-            nc.sync.dma_start(out=out[:, lo : lo + 3 * P], in_=res[:])

@@ -34,7 +34,7 @@ def tile_attend_brankshares_heads_kernel(tc, hid, voc_words, voc_scales, sw, old
         psum = ctx.enter_context(tc.psum_pool(name="psum", bufs=1))
 
         planes = keep.tile([P, BANK], U8, align_bytes=64)
-        nc.vector.memset(planes[:].bitcast(U32), 0)
+        nc.gpsimd.memset(planes[:].bitcast(U32), 0)
 
         raw = keep.tile([P, PACK, Q], F32, tag="raw")
         nc.sync.dma_start(out=raw[:], in_=hid.rearrange("(p j) q -> p j q", j=PACK))
@@ -56,16 +56,16 @@ def tile_attend_brankshares_heads_kernel(tc, hid, voc_words, voc_scales, sw, old
         nc.sync.dma_start(list2[:], offs2)
 
         up = keep.tile([P, V], F32)
-        down = keep.tile([P, V], F32)
         nc.vector.memset(up[:], 0.0)
-        nc.vector.memset(down[:], 0.0)
         fac = keep.tile([P, nch], F32)
         nc.vector.memset(fac[:, nch - 1 : nch], 1.0)
         ident = keep.tile([P, P], F32)
         make_identity(nc, ident[:])
 
         grouped = keep.tile([P, Q, PACK], BF16, align_bytes=64, tag="grouped")
-        nc.vector.tensor_copy(out=grouped[:], in_=raw[:].rearrange("p j q -> p q j"))
+        half = Q // 2
+        nc.vector.tensor_copy(out=grouped[:, :half, :], in_=raw[:, :, :half].rearrange("p j q -> p q j"))
+        nc.scalar.copy(out=grouped[:, half:, :], in_=raw[:, :, half:].rearrange("p j q -> p q j"))
         hcodes = keep.tile([P, Q], U32, align_bytes=64)
         hscales = keep.tile([P, Q], U8, align_bytes=64)
         nc.vector.quantize_mx(
@@ -138,7 +138,7 @@ def tile_attend_brankshares_heads_kernel(tc, hid, voc_words, voc_scales, sw, old
         for lo, hi in HALVES:
             nc.scalar.activation(px[:, lo:hi], a1[:, lo:hi], ACT.Exp, bias=neg_m[:])
             nc.vector.tensor_tensor(diff[:, lo:hi], px2[:, lo:hi], px[:, lo:hi], ALU.subtract)
-        wd = keep.tile([P, SLOTS], F32)
+        wd = keep.tile([P, SLOTS], F32, tag="wd")
         for lo, hi in HALVES:
             nc.vector.tensor_tensor(wd[:, lo:hi], diff[:, lo:hi], swk_flat[:, lo:hi], ALU.mult)
         for h, (lo, hi) in enumerate(HALVES):
@@ -150,6 +150,8 @@ def tile_attend_brankshares_heads_kernel(tc, hid, voc_words, voc_scales, sw, old
             nc.vector.scalar_tensor_tensor(
                 gd[:, lo:hi], sq[:, lo:hi], -1.0, wd[:, lo:hi], ALU.add, ALU.mult, accum_out=rr[:, h : h + 1]
             )
+        down = keep.tile([P, V], F32, tag="wd")
+        nc.gpsimd.memset(down[:], 0.0)
         nc.vector.tensor_tensor(up[:].indirect(list2[:]), g[:], px2[:], ALU.mult)
         nc.vector.tensor_tensor(down[:].indirect(list1[:]), g[:], px[:], ALU.mult)
 

@@ -21,9 +21,9 @@ P = 128
 PACK = 4
 BANK = 512
 NBANK = V // BANK
-WORD_LOADS = ((0, 512), (512, 1024), (1024, 2048))
+WORD_LOADS = ((0, 512), (512, 1024), (1024, 1536), (1536, 2048))
 CHUNKS = ((0, 256), (256, 512), (512, 1024), (1024, 1536), (1536, 2048))
-HALVES = ((0, 256), (256, 512))
+HALVES = ((0, 128), (128, 256), (256, 384), (384, 512))
 
 
 def tile_attend_brankshares_heads_kernel(tc, hid, voc_words, voc_scales, sw, old, offs, offs2, out):
@@ -34,7 +34,6 @@ def tile_attend_brankshares_heads_kernel(tc, hid, voc_words, voc_scales, sw, old
         psum = ctx.enter_context(tc.psum_pool(name="psum", bufs=1))
 
         planes = keep.tile([P, BANK], U8, align_bytes=64)
-        nc.gpsimd.memset(planes[:].bitcast(U32), 0)
 
         raw = keep.tile([P, PACK, Q], F32, tag="raw")
         nc.sync.dma_start(out=raw[:], in_=hid.rearrange("(p j) q -> p j q", j=PACK))
@@ -129,7 +128,7 @@ def tile_attend_brankshares_heads_kernel(tc, hid, voc_words, voc_scales, sw, old
         nc.vector.tensor_scalar(fk[:], fac[:], k[:], -1.0 / 256.0, ALU.mult, ALU.mult)
 
         px = keep.tile([P, SLOTS], F32)
-        diff = keep.tile([P, SLOTS], F32)
+        diff = keep.tile([P, SLOTS], F32, tag="wd")
         th = keep.tile([P, SLOTS], F32)
         sq = keep.tile([P, SLOTS], F32)
         g = keep.tile([P, SLOTS], F32)
@@ -138,9 +137,6 @@ def tile_attend_brankshares_heads_kernel(tc, hid, voc_words, voc_scales, sw, old
         for lo, hi in HALVES:
             nc.scalar.activation(px[:, lo:hi], a1[:, lo:hi], ACT.Exp, bias=neg_m[:])
             nc.vector.tensor_tensor(diff[:, lo:hi], px2[:, lo:hi], px[:, lo:hi], ALU.subtract)
-        wd = keep.tile([P, SLOTS], F32, tag="wd")
-        for lo, hi in HALVES:
-            nc.vector.tensor_tensor(wd[:, lo:hi], diff[:, lo:hi], swk_flat[:, lo:hi], ALU.mult)
         for h, (lo, hi) in enumerate(HALVES):
             nc.scalar.activation(th[:, lo:hi], diff[:, lo:hi], ACT.Tanh, scale=k[:])
             nc.scalar.activation(sq[:, lo:hi], th[:, lo:hi], ACT.Square)
@@ -148,7 +144,7 @@ def tile_attend_brankshares_heads_kernel(tc, hid, voc_words, voc_scales, sw, old
                 g[:, lo:hi], sq[:, lo:hi], -1.0, swk_flat[:, lo:hi], ALU.add, ALU.mult
             )
             nc.vector.scalar_tensor_tensor(
-                gd[:, lo:hi], sq[:, lo:hi], -1.0, wd[:, lo:hi], ALU.add, ALU.mult, accum_out=rr[:, h : h + 1]
+                gd[:, lo:hi], g[:, lo:hi], 1.0, diff[:, lo:hi], ALU.mult, ALU.mult, accum_out=rr[:, h : h + 1]
             )
         down = keep.tile([P, V], F32, tag="wd")
         nc.gpsimd.memset(down[:], 0.0)
@@ -156,51 +152,72 @@ def tile_attend_brankshares_heads_kernel(tc, hid, voc_words, voc_scales, sw, old
         nc.vector.tensor_tensor(down[:].indirect(list1[:]), g[:], px[:], ALU.mult)
 
         r = keep.tile([P, 1], F32)
-        nc.scalar.activation(r[:], rr[:, 0:1], ACT.Identity, bias=rr[:, 1:2])
+        rr_copy = keep.tile([P, len(HALVES)], F32)
+        nc.scalar.activation(rr_copy[:], rr[:], ACT.Copy, accum_out=r[:])
         cvec = keep.tile([P, nch], F32)
         nc.scalar.activation(cvec[:], fk[:], ACT.Copy, scale=r[:])
         cp = keep.tile([P, V], F32)
+        dlo, dhi = 9 * P, 12 * P
+        dchunk = 3
         for c, (lo, hi) in enumerate(CHUNKS):
+            hi = dlo if c == dchunk else hi
             nc.scalar.activation(cp[:, lo:hi], p_sb[:, lo:hi], ACT.Copy, scale=cvec[:, c : c + 1])
 
-        turned = [psum.tile([P, BANK], F32, tag="bank%d" % ((6 + b) % 8), name="turned%d" % b) for b in range(NBANK)]
-
-        def blocks(b):
-            return [3 * b, 3 * b + 1, 3 * b + 2, 12 + b]
+        bank_blocks = ((0, 1, 2, 12), (3, 4, 5, 13), (6, 7, 8, 14), (15,))
+        turned = [
+            psum.tile([P, len(bank_blocks[b]) * P], F32, tag="bank%d" % ((6 + b) % 8), name="turned%d" % b)
+            for b in range(NBANK)
+        ]
 
         def add_turned(src, b, places, first, last):
             for j in places:
-                blk = blocks(b)[j]
+                blk = bank_blocks[b][j]
                 nc.tensor.matmul(
                     turned[b][:, j * P : (j + 1) * P],
                     lhsT=src[:, blk * P : (blk + 1) * P],
                     rhs=ident[:],
                     is_transpose=True,
                     start=(first and j == 0),
-                    stop=(last and j == 3),
+                    stop=(last and j == len(bank_blocks[b]) - 1),
                 )
 
         for b in range(NBANK):
-            add_turned(old_sb, b, range(4), True, False)
+            add_turned(old_sb, b, range(len(bank_blocks[b])), True, False)
         for b in range(NBANK):
-            add_turned(cp, b, range(3), False, False)
+            add_turned(cp, b, range(len(bank_blocks[b]) - 1), False, False)
         for b in range(NBANK):
-            add_turned(cp, b, (3,), False, False)
+            add_turned(cp, b, (len(bank_blocks[b]) - 1,), False, False)
+
+        rest = keep.tile([P, dhi - dlo], F32)
+        nc.gpsimd.tensor_tensor(rest[:], old_sb[:, dlo:dhi], down[:, dlo:dhi], ALU.subtract)
+        nc.gpsimd.tensor_tensor(rest[:], rest[:], up[:, dlo:dhi], ALU.add)
+
         res_last = [keep.tile([P, 2 * P], F32, name="res_last%d" % h) for h in range(2)]
         for b in range(NBANK):
-            add_turned(up, b, range(4), False, True)
-            turned_sb = keep.tile([P, BANK], F32, name="turned_sb%d" % b)
+            n = len(bank_blocks[b])
+            add_turned(up, b, range(n), False, True)
+            turned_sb = keep.tile([P, n * P], F32, name="turned_sb%d" % b, tag="turned_sb%d" % b)
             nc.scalar.copy(turned_sb[:], turned[b][:])
-            back = psum.tile([P, BANK], F32, tag="bank%d" % (2 + b), name="back%d" % b)
-            for j in range(BANK // P):
+            back = psum.tile([P, n * P], F32, tag="bank%d" % (2 + b), name="back%d" % b)
+            for j in range(n):
                 nc.tensor.transpose(back[:, j * P : (j + 1) * P], turned_sb[:, j * P : (j + 1) * P], ident[:])
-            res = keep.tile([P, 3 * P], F32, name="res%d" % b)
-            lo = 3 * b * P
-            nc.vector.tensor_tensor(res[:], back[:, : 3 * P], down[:, lo : lo + 3 * P], ALU.subtract)
-            nc.sync.dma_start(out=out[:, lo : lo + 3 * P], in_=res[:])
-            lo = (12 + b) * P
+            if n > 1:
+                res = keep.tile([P, (n - 1) * P], F32, name="res%d" % b)
+                lo = bank_blocks[b][0] * P
+                hi = lo + (n - 1) * P
+                nc.vector.tensor_tensor(res[:], back[:, : (n - 1) * P], down[:, lo:hi], ALU.subtract)
+                nc.sync.dma_start(out=out[:, lo:hi], in_=res[:])
+            lo = bank_blocks[b][-1] * P
             nc.vector.tensor_tensor(
-                res_last[b // 2][:, (b % 2) * P : (b % 2 + 1) * P], back[:, 3 * P :], down[:, lo : lo + P], ALU.subtract
+                res_last[b // 2][:, (b % 2) * P : (b % 2 + 1) * P],
+                back[:, (n - 1) * P :],
+                down[:, lo : lo + P],
+                ALU.subtract,
             )
             if b % 2 == 1:
                 nc.sync.dma_start(out=out[:, lo - P : lo + P], in_=res_last[b // 2][:])
+        res_direct = keep.tile([P, dhi - dlo], F32, tag="turned_sb2")
+        nc.vector.scalar_tensor_tensor(
+            res_direct[:], p_sb[:, dlo:dhi], cvec[:, dchunk : dchunk + 1], rest[:], ALU.mult, ALU.add
+        )
+        nc.sync.dma_start(out=out[:, dlo:dhi], in_=res_direct[:])

from contextlib import ExitStack

import concourse.mybir as mybir
from concourse.masks import make_identity

D, V, Q, SLOTS = 512, 2048, 128, 512
FLOPS = 2 * D * V * Q

F32 = mybir.dt.float32
BF16 = mybir.dt.bfloat16
I32 = mybir.dt.int32
U32 = mybir.dt.uint32
U16 = mybir.dt.uint16
U8 = mybir.dt.uint8
FP8X4 = mybir.dt.float8_e4m3fn_x4
ALU = mybir.AluOpType
ACT = mybir.ActivationFunctionType
AX = mybir.AxisListType

P = 128
PACK = 4
BANK = 512
NBANK = V // BANK
WORD_LOADS = ((0, 512), (512, 1024), (1024, 1536), (1536, 2048))
CHUNKS = ((0, 256), (256, 512), (512, 1024), (1024, 1536), (1536, 2048))
HALVES = ((0, 128), (128, 256), (256, 384), (384, 512))


def tile_attend_brankshares_heads_kernel(tc, hid, voc_words, voc_scales, sw, old, offs, offs2, out):
    nc = tc.nc
    nch = len(CHUNKS)
    with ExitStack() as ctx:
        keep = ctx.enter_context(tc.tile_pool(name="keep", bufs=1))
        psum = ctx.enter_context(tc.psum_pool(name="psum", bufs=1))

        planes = keep.tile([P, BANK], U8, align_bytes=64)

        raw = keep.tile([P, PACK, Q], F32, tag="raw")
        nc.sync.dma_start(out=raw[:], in_=hid.rearrange("(p j) q -> p j q", j=PACK))
        for quad in range(4):
            rows = voc_scales[0][4 * quad : 4 * quad + 4, :].bitcast(I32)
            nc.sync.dma_start(
                out=planes[32 * quad : 32 * quad + 16, :].bitcast(I32),
                in_=rows.rearrange("r (c n) -> c r n", c=NBANK),
            )
        flat_words = voc_words[0].rearrange("p n t -> p (n t)")
        words = []
        for lo, hi in WORD_LOADS:
            w = keep.tile([P, hi - lo], U32, align_bytes=64, name="words%d" % lo)
            nc.sync.dma_start(out=w[:].bitcast(I32), in_=flat_words[:, PACK * lo : PACK * hi].bitcast(I32))
            words.append((lo, hi, w))
        list1 = keep.tile([P, SLOTS // 16], U16)
        nc.sync.dma_start(list1[:], offs)
        list2 = keep.tile([P, SLOTS // 16], U16)
        nc.sync.dma_start(list2[:], offs2)

        up = keep.tile([P, V], F32)
        nc.vector.memset(up[:], 0.0)
        fac = keep.tile([P, nch], F32)
        nc.vector.memset(fac[:, nch - 1 : nch], 1.0)
        ident = keep.tile([P, P], F32)
        make_identity(nc, ident[:])

        grouped = keep.tile([P, Q, PACK], BF16, align_bytes=64, tag="grouped")
        half = Q // 2
        nc.vector.tensor_copy(out=grouped[:, :half, :], in_=raw[:, :, :half].rearrange("p j q -> p q j"))
        nc.scalar.copy(out=grouped[:, half:, :], in_=raw[:, :, half:].rearrange("p j q -> p q j"))
        hcodes = keep.tile([P, Q], U32, align_bytes=64)
        hscales = keep.tile([P, Q], U8, align_bytes=64)
        nc.vector.quantize_mx(
            out=hcodes[:].bitcast(FP8X4), scales=hscales[:], in_=grouped[:].rearrange("p q j -> p (q j)")
        )

        sw_col = keep.tile([P, PACK], F32, tag="raw")
        nc.sync.dma_start(out=sw_col[:], in_=sw[0].rearrange("(p c) -> p c", c=PACK))
        old_sb = keep.tile([P, V], F32, align_bytes=64, tag="grouped")
        nc.sync.dma_start(out=old_sb[:], in_=old)

        a_sb = keep.tile([P, V], F32)
        p_sb = keep.tile([P, V], F32)
        mx = keep.tile([P, nch], F32)
        neg = keep.tile([P, nch - 1], F32)
        neg_m = keep.tile([P, 1], F32)
        zc = keep.tile([P, nch], F32)
        for c, (lo, hi) in enumerate(CHUNKS):
            wlo, whi, w = [t for t in words if t[0] <= lo and hi <= t[1]][0]
            b = lo // BANK
            acc = psum.tile([P, hi - lo], F32, tag="bank%d" % c, name="acc%d" % c)
            nc.tensor.matmul_mx(
                out=acc[:],
                lhsT=hcodes[:].bitcast(FP8X4),
                lhsT_scale=hscales[:],
                rhs=w[:, lo - wlo : hi - wlo].bitcast(FP8X4),
                rhs_scale=planes[4 * b :, lo - b * BANK : hi - b * BANK],
                start=True,
                stop=True,
            )
            nc.vector.tensor_scalar(
                a_sb[:, lo:hi], acc[:], 1.0, None, ALU.mult, ALU.max, accum_out=mx[:, c : c + 1]
            )
            if c < nch - 1:
                nc.gpsimd.tensor_scalar(neg[:, c : c + 1], mx[:, c : c + 1], -1.0, 0.0, ALU.mult, ALU.add)
                bias = neg[:, c : c + 1]
            else:
                nc.vector.tensor_reduce(neg_m[:], mx[:], AX.X, ALU.max, negate=True)
                bias = neg_m[:]
            nc.scalar.activation(p_sb[:, lo:hi], a_sb[:, lo:hi], ACT.Exp, bias=bias, accum_out=zc[:, c : c + 1])

        nc.scalar.activation(fac[:, : nch - 1], mx[:, : nch - 1], ACT.Exp, bias=neg_m[:])
        px2 = keep.tile([P, SLOTS], F32)
        nc.scalar.activation(px2[:], a_sb[:].indirect(list2[:]), ACT.Exp, bias=neg_m[:])
        a1 = keep.tile([P, SLOTS], F32)
        nc.vector.tensor_copy(a1[:], a_sb[:].indirect(list1[:]))

        sw_ps = psum.tile([P, PACK, P], F32, tag="bank5")
        for c in range(PACK):
            nc.tensor.transpose(sw_ps[:, c, :], sw_col[:, c : c + 1].to_broadcast([P, P]), ident[:])

        zf = keep.tile([P, nch], F32)
        z256 = keep.tile([P, 1], F32)
        nc.vector.scalar_tensor_tensor(zf[:], zc[:], 1.0 / 256.0, fac[:], ALU.mult, ALU.mult, accum_out=z256[:])
        k = keep.tile([P, 1], F32)
        nc.vector.reciprocal(k[:], z256[:])
        swk = keep.tile([P, P, PACK], F32)
        nc.vector.tensor_scalar(swk[:], sw_ps[:].rearrange("q c p -> q p c"), k[:], -1.0, ALU.mult, ALU.mult)
        swk_flat = swk[:].rearrange("q p c -> q (p c)")
        fk = keep.tile([P, nch], F32)
        nc.vector.tensor_scalar(fk[:], fac[:], k[:], -1.0 / 256.0, ALU.mult, ALU.mult)

        px = keep.tile([P, SLOTS], F32)
        diff = keep.tile([P, SLOTS], F32, tag="wd")
        th = keep.tile([P, SLOTS], F32)
        sq = keep.tile([P, SLOTS], F32)
        g = keep.tile([P, SLOTS], F32)
        gd = keep.tile([P, SLOTS], F32)
        rr = keep.tile([P, len(HALVES)], F32)
        for lo, hi in HALVES:
            nc.scalar.activation(px[:, lo:hi], a1[:, lo:hi], ACT.Exp, bias=neg_m[:])
            nc.vector.tensor_tensor(diff[:, lo:hi], px2[:, lo:hi], px[:, lo:hi], ALU.subtract)
        for h, (lo, hi) in enumerate(HALVES):
            nc.scalar.activation(th[:, lo:hi], diff[:, lo:hi], ACT.Tanh, scale=k[:])
            nc.scalar.activation(sq[:, lo:hi], th[:, lo:hi], ACT.Square)
            nc.vector.scalar_tensor_tensor(
                g[:, lo:hi], sq[:, lo:hi], -1.0, swk_flat[:, lo:hi], ALU.add, ALU.mult
            )
            nc.vector.scalar_tensor_tensor(
                gd[:, lo:hi], g[:, lo:hi], 1.0, diff[:, lo:hi], ALU.mult, ALU.mult, accum_out=rr[:, h : h + 1]
            )
        down = keep.tile([P, V], F32, tag="wd")
        nc.gpsimd.memset(down[:], 0.0)
        nc.vector.tensor_tensor(up[:].indirect(list2[:]), g[:], px2[:], ALU.mult)
        nc.vector.tensor_tensor(down[:].indirect(list1[:]), g[:], px[:], ALU.mult)

        r = keep.tile([P, 1], F32)
        rr_copy = keep.tile([P, len(HALVES)], F32)
        nc.scalar.activation(rr_copy[:], rr[:], ACT.Copy, accum_out=r[:])
        cvec = keep.tile([P, nch], F32)
        nc.scalar.activation(cvec[:], fk[:], ACT.Copy, scale=r[:])
        cp = keep.tile([P, V], F32)
        dlo, dhi = 9 * P, 12 * P
        dchunk = 3
        for c, (lo, hi) in enumerate(CHUNKS):
            hi = dlo if c == dchunk else hi
            nc.scalar.activation(cp[:, lo:hi], p_sb[:, lo:hi], ACT.Copy, scale=cvec[:, c : c + 1])

        bank_blocks = ((0, 1, 2, 12), (3, 4, 5, 13), (6, 7, 8, 14), (15,))
        turned = [
            psum.tile([P, len(bank_blocks[b]) * P], F32, tag="bank%d" % ((6 + b) % 8), name="turned%d" % b)
            for b in range(NBANK)
        ]

        def add_turned(src, b, places, first, last):
            for j in places:
                blk = bank_blocks[b][j]
                nc.tensor.matmul(
                    turned[b][:, j * P : (j + 1) * P],
                    lhsT=src[:, blk * P : (blk + 1) * P],
                    rhs=ident[:],
                    is_transpose=True,
                    start=(first and j == 0),
                    stop=(last and j == len(bank_blocks[b]) - 1),
                )

        for b in range(NBANK):
            add_turned(old_sb, b, range(len(bank_blocks[b])), True, False)
        for b in range(NBANK):
            add_turned(cp, b, range(len(bank_blocks[b]) - 1), False, False)
        for b in range(NBANK):
            add_turned(cp, b, (len(bank_blocks[b]) - 1,), False, False)

        rest = keep.tile([P, dhi - dlo], F32)
        nc.gpsimd.tensor_tensor(rest[:], old_sb[:, dlo:dhi], down[:, dlo:dhi], ALU.subtract)
        nc.gpsimd.tensor_tensor(rest[:], rest[:], up[:, dlo:dhi], ALU.add)

        res_last = [keep.tile([P, 2 * P], F32, name="res_last%d" % h) for h in range(2)]
        for b in range(NBANK):
            n = len(bank_blocks[b])
            add_turned(up, b, range(n), False, True)
            turned_sb = keep.tile([P, n * P], F32, name="turned_sb%d" % b, tag="turned_sb%d" % b)
            nc.scalar.copy(turned_sb[:], turned[b][:])
            back = psum.tile([P, n * P], F32, tag="bank%d" % (2 + b), name="back%d" % b)
            for j in range(n):
                nc.tensor.transpose(back[:, j * P : (j + 1) * P], turned_sb[:, j * P : (j + 1) * P], ident[:])
            if n > 1:
                res = keep.tile([P, (n - 1) * P], F32, name="res%d" % b)
                lo = bank_blocks[b][0] * P
                hi = lo + (n - 1) * P
                nc.vector.tensor_tensor(res[:], back[:, : (n - 1) * P], down[:, lo:hi], ALU.subtract)
                nc.sync.dma_start(out=out[:, lo:hi], in_=res[:])
            lo = bank_blocks[b][-1] * P
            nc.vector.tensor_tensor(
                res_last[b // 2][:, (b % 2) * P : (b % 2 + 1) * P],
                back[:, (n - 1) * P :],
                down[:, lo : lo + P],
                ALU.subtract,
            )
            if b % 2 == 1:
                nc.sync.dma_start(out=out[:, lo - P : lo + P], in_=res_last[b // 2][:])
        res_direct = keep.tile([P, dhi - dlo], F32, tag="turned_sb2")
        nc.vector.scalar_tensor_tensor(
            res_direct[:], p_sb[:, dlo:dhi], cvec[:, dchunk : dchunk + 1], rest[:], ALU.mult, ALU.add
        )
        nc.sync.dma_start(out=out[:, dlo:dhi], in_=res_direct[:])
